import numpy as np
import ml_dtypes


def mxq(x, axis, fmt="e4m3"):
    dtype, down = {"e4m3": (ml_dtypes.float8_e4m3fn, 7), "e5m2": (ml_dtypes.float8_e5m2, 14)}[fmt]
    v = np.moveaxis(np.asarray(x, np.float32).astype(ml_dtypes.bfloat16).astype(np.float64), axis, -1)
    blocks = v.reshape(v.shape[:-1] + (-1, 32))
    amax = np.abs(blocks).max(-1, keepdims=True)
    byte = np.maximum(np.where(amax > 0, np.frexp(amax)[1] - 1 + 127, 0) - down, 1)
    scale = np.exp2(byte - 127.0)
    codes = (blocks / scale).astype(np.float32).astype(dtype).astype(np.float64)
    return np.moveaxis((codes * scale).reshape(v.shape), -1, axis)


WIDE = False


def mx_kscale(k):
    if not WIDE:
        return np.ones(k)
    levels = np.array([30, -30])
    if k % 512:
        return np.exp2(np.random.permutation(np.resize(levels, k // 32))).repeat(32)
    a = np.empty((k // 512, 16))
    for p in range(k // 512):
        a[p, :8] = np.random.permutation(np.resize(levels, 8))
        for g in range(8):
            far = levels[np.abs(levels - a[p, g]) >= 10]
            a[p, g + 8] = far[np.random.randint(len(far))]
    return np.exp2(a.ravel()).repeat(32)


def f64(x):
    return np.asarray(x).astype(np.float64)


def striped(idx):
    return np.tile(np.asarray(idx).reshape(-1, 16).T, (8, 1)).astype(np.uint16)


def unstriped(offs):
    return offs[:16].T.reshape(-1).astype(np.int64)


E2M1 = np.array([0.0, 0.5, 1.0, 1.5, 2.0, 3.0, 4.0, 6.0, -0.0, -0.5, -1.0, -1.5, -2.0, -3.0, -4.0, -6.0])


def pack_weight(w, fmt):
    k, n = w.shape
    w = f64(np.asarray(w, np.float32).astype(ml_dtypes.bfloat16)).reshape(k // 32, 32, n)
    amax = np.abs(w).max(1)
    if fmt in ("e4m3", "e5m2"):
        byte = np.frexp(amax)[1] - 1 + 127 - (7 if fmt == "e4m3" else 14)
    else:
        mant, ex = np.frexp(amax / 6.0)
        byte = np.where(mant > 0.5, ex, ex - 1) + 127
    byte = np.clip(np.where(amax > 0, byte, 1), 1, 254)
    scaled = (w * np.exp2(127.0 - byte)[:, None, :]).reshape(k, n).astype(np.float32)
    by_word = np.ascontiguousarray(scaled.reshape(k // 512, 128, 4, n).transpose(0, 1, 3, 2))
    if fmt in ("e4m3", "e5m2"):
        words = by_word.astype(ml_dtypes.float8_e4m3fn if fmt == "e4m3" else ml_dtypes.float8_e5m2).view(np.uint8)
    else:
        c = by_word.astype(ml_dtypes.float4_e2m1fn).view(np.uint8) & 0xF
        words = (c[..., 0::2] | (c[..., 1::2] << 4)).reshape(k // 512, 128, 2 * n)
    return np.ascontiguousarray(words), np.ascontiguousarray(byte.astype(np.uint8).reshape(k // 512, 16, n))


def unpack_weight(words, scales, fmt):
    g, _, n = scales.shape
    words = np.ascontiguousarray(words).reshape(g, 128, n, -1)
    if fmt in ("e4m3", "e5m2"):
        vals = words.view(ml_dtypes.float8_e4m3fn if fmt == "e4m3" else ml_dtypes.float8_e5m2).astype(np.float64)
    else:
        nib = np.empty((g, 128, n, 4), np.uint8)
        nib[..., 0::2] = words & 0xF
        nib[..., 1::2] = words >> 4
        vals = E2M1[nib]
    vals = vals * np.repeat(np.exp2(scales.astype(np.float64) - 127.0), 8, axis=1)[..., None]
    return vals.transpose(0, 1, 3, 2).reshape(g * 512, n)


K, T, J, I, R, V = 512, 512, 256, 256, 512, 512


def setup_inputs():
    n = np.random.standard_normal
    idx = np.random.permutation(T)[:J]
    idx2 = np.random.permutation(T)[:I]
    idx3 = np.random.permutation(V)[:I]
    fk = mx_kscale(K)
    fr = mx_kscale(R)
    xtp = pack_weight(n((K, T)) / fk[:, None], "e4m3")
    wap = pack_weight(n((K, R)) * 0.5 / np.sqrt(K) * fk[:, None] * fr, "e5m2")
    wbp = pack_weight(n((K, R)) * 1 / np.sqrt(K) * fk[:, None] / fr, "e2m1")
    return {
        "xt_words": xtp[0],
        "xt_scales": xtp[1],
        "wa_words": wap[0],
        "wa_scales": wap[1],
        "oa": (n((R, J)) * 0.5 * fr[:, None]).astype(np.float32),
        "wb_words": wbp[0],
        "wb_scales": wbp[1],
        "tb": (n((R, V)) * 0.5 / fr[:, None]).astype(np.float32),
        "offs": striped(idx),
        "offs2": striped(idx2),
        "offs3": striped(idx3),
    }


def reference(xt_words, xt_scales, wa_words, wa_scales, oa, wb_words, wb_scales, tb, offs, offs2, offs3):
    idx = unstriped(offs)
    idx2 = unstriped(offs2)
    idx3 = unstriped(offs3)
    xtu = unpack_weight(xt_words, xt_scales, "e4m3")
    wau = unpack_weight(wa_words, wa_scales, "e5m2")
    wbu = unpack_weight(wb_words, wb_scales, "e2m1")
    xtidxg = xtu[:, idx]
    za = wau.T @ xtidxg
    ha = np.maximum(za, f64(oa))
    xtidx2g = xtu[:, idx2]
    zb = wbu.T @ xtidx2g
    hb = np.maximum(zb - f64(tb)[:, idx3], 0.0)
    haq = mxq(ha, 0, "e4m3")
    hbq = mxq(hb, 0, "e5m2")
    a0 = haq.T @ hbq
    mn = np.mean(a0, axis=1, keepdims=True)
    y = 0.04 * np.maximum(a0 - mn, 0.0)
    return y

@@ -1,0 +1,192 @@
+from contextlib import ExitStack
+
+import concourse.mybir as mybir
+
+K, T, J, I, R, V = 512, 512, 256, 256, 512, 512
+FLOPS = 2 * K * R * (J + I) + 2 * R * J * I
+
+F32 = mybir.dt.float32
+BF16 = mybir.dt.bfloat16
+I32 = mybir.dt.int32
+U32 = mybir.dt.uint32
+U16 = mybir.dt.uint16
+U8 = mybir.dt.uint8
+E4M3 = mybir.dt.float8_e4m3fn_x4
+E5M2 = mybir.dt.float8_e5m2_x4
+E2M1 = mybir.dt.float4_e2m1fn_x4
+ALU = mybir.AluOpType
+ACT = mybir.ActivationFunctionType
+
+P = 128
+PACK = 4
+HALF = 128
+KEEP = 0.04
+
+
+def load_scale_rows_filling(queue, plane, scales):
+    rows = scales[0].bitcast(I32).rearrange("(q o r) c -> q o r c", o=1, r=4)
+    for q in range(4):
+        queue.dma_start(plane[32 * q : 32 * (q + 1), :].bitcast(I32), rows[q].broadcast_to([8, 4, rows.shape[3]]))
+
+
+def load_scale_rows(queue, plane, scales):
+    rows = scales[0].bitcast(I32)
+    for q in range(4):
+        queue.dma_start(plane[32 * q : 32 * q + 4, :].bitcast(I32), rows[4 * q : 4 * q + 4, :])
+
+
+def deal_columns(copy, dealt, given):
+    copy(
+        dealt.rearrange("p (t c i) -> p c t i", t=PACK, i=4),
+        given.rearrange("p (c i t) -> p c t i", t=PACK, i=4),
+    )
+
+
+def deal_bytes(nc, dealt, given):
+    nc.vector.tensor_copy(
+        dealt.rearrange("p (t c i) -> p c t i", t=PACK, i=16),
+        given.rearrange("p (c i t) -> p c t i", t=PACK, i=16),
+    )
+
+
+def tile_list_meet_added_overtable_abovemean_kernel(
+    tc, xt_words, xt_scales, wa_words, wa_scales, oa, wb_words, wb_scales, tb, offs, offs2, offs3, out
+):
+    nc = tc.nc
+    with ExitStack() as ctx:
+        sb = ctx.enter_context(tc.tile_pool(name="sb", bufs=1))
+        ps = ctx.enter_context(tc.psum_pool(name="ps", bufs=1))
+
+        list_a = sb.tile([P, J // 16], U16, name="list_a")
+        list_b = sb.tile([P, I // 16], U16, name="list_b")
+        list_t = sb.tile([P, I // 16], U16, name="list_t")
+        x_scales = sb.tile([P, T], U8, name="x_scales", align_bytes=64)
+        x_words = sb.tile([P, T], I32, name="x_words", align_bytes=64)
+        wa_given = sb.tile([P, R], I32, name="wa_given", align_bytes=64)
+        wb_given = sb.tile([P, R // 2], I32, name="wb_given", tag="wb_then_picked", align_bytes=64)
+        wa_scales_given = sb.tile([P, R], U8, name="wa_scales_given", tag="wa_scales_then_diff", align_bytes=64)
+        wb_scales_given = sb.tile([P, R], U8, name="wb_scales_given", align_bytes=64)
+        tb_pairs = [sb.tile([P, 2 * V], F32, name="tb_pair%d" % u, align_bytes=64) for u in range(2)]
+        oa_halves = [sb.tile([P, PACK, HALF], F32, name="oa_half%d" % h, tag="oa_half%d" % h, align_bytes=64) for h in range(2)]
+
+        tb_rows = tb.rearrange("(p t) v -> p (t v)", t=PACK)
+        oa_rows = oa.rearrange("(p t) j -> p t j", t=PACK)
+
+        nc.vector.memset(wb_scales_given[:].bitcast(I32), 0)
+        nc.vector.memset(wa_scales_given[:].bitcast(I32), 0)
+        nc.sync.dma_start(list_b[:], offs2)
+        nc.sync.dma_start(x_words[:], xt_words[0].rearrange("p c r -> p (c r)").bitcast(I32))
+        nc.sync.dma_start(list_a[:], offs)
+        load_scale_rows_filling(nc.sync, x_scales, xt_scales)
+        nc.sync.dma_start(tb_pairs[0][:], tb_rows[:, 0 : 2 * V])
+        nc.sync.dma_start(list_t[:], offs3)
+        nc.sync.dma_start(wb_given[:], wb_words[0].bitcast(I32))
+        load_scale_rows(nc.sync, wb_scales_given, wb_scales)
+        nc.sync.dma_start(tb_pairs[1][:], tb_rows[:, 2 * V : 4 * V])
+        nc.sync.dma_start(wa_given[:], wa_words[0].rearrange("p c r -> p (c r)").bitcast(I32))
+        load_scale_rows(nc.sync, wa_scales_given, wa_scales)
+        for h in range(2):
+            nc.sync.dma_start(oa_halves[h][:], oa_rows[:, :, h * HALF : (h + 1) * HALF])
+
+        xb_scales = sb.tile([P, I], U8, name="xb_scales", align_bytes=64)
+        xb_words = sb.tile([P, I], U32, name="xb_words", align_bytes=64)
+        xa_scales = sb.tile([P, J], U8, name="xa_scales", align_bytes=64)
+        xa_words = sb.tile([P, J], U32, name="xa_words", align_bytes=64)
+        wa_dealt = sb.tile([P, R], U32, name="wa_dealt", align_bytes=64)
+        wa_scales_dealt = sb.tile([P, R], U8, name="wa_scales_dealt", align_bytes=64)
+        wb_scales_dealt = sb.tile([P, R], U8, name="wb_scales_dealt", align_bytes=64)
+
+        nc.vector.tensor_copy(xb_words[:], x_words[:].bitcast(U32).indirect(list_b[:]))
+        nc.vector.tensor_copy(xa_words[:], x_words[:].bitcast(U32).indirect(list_a[:]))
+        nc.vector.tensor_copy(xb_scales[:], x_scales[:].indirect(list_b[:]))
+        nc.vector.tensor_copy(xa_scales[:], x_scales[:].indirect(list_a[:]))
+        deal_bytes(nc, wb_scales_dealt[:], wb_scales_given[:])
+        wb_dealt = sb.tile([P, R], U16, name="wb_dealt", align_bytes=64)
+        deal_columns(nc.scalar.copy, wb_dealt[:], wb_given[:].bitcast(U16))
+        zb = [ps.tile([P, 2, I], F32, name="zb%d" % u) for u in range(2)]
+        wb_bytes = wb_dealt[:].bitcast(U8)
+        for t in range(PACK):
+            nc.tensor.matmul_mx(
+                out=zb[t // 2][:, t % 2, :],
+                lhsT=wb_bytes[:, 2 * t * P : 2 * (t + 1) * P].bitcast(E2M1),
+                lhsT_scale=wb_scales_dealt[:, t * P : (t + 1) * P],
+                rhs=xb_words[:].bitcast(E4M3),
+                rhs_scale=xb_scales[:],
+                start=True,
+                stop=True,
+            )
+
+
+        picked = sb.tile([P, PACK, I], F32, name="picked", tag="wb_then_picked", align_bytes=64)
+        for t in range(PACK):
+            window = tb_pairs[t // 2][:, (t % 2) * V : (t % 2 + 1) * V]
+            nc.scalar.activation(picked[:, t, :], window.indirect(list_t[:]), ACT.Copy)
+        deal_columns(nc.vector.tensor_copy, wa_dealt[:].bitcast(I32), wa_given[:])
+        deal_bytes(nc, wa_scales_dealt[:], wa_scales_given[:])
+        diff = sb.tile([P, PACK, I], F32, name="diff", tag="wa_scales_then_diff", align_bytes=64)
+        nc.vector.tensor_tensor(diff[:, 0:2, :], zb[0][:], picked[:, 0:2, :], ALU.subtract)
+        for t in (2, 3):
+            nc.vector.tensor_tensor(diff[:, t, :], zb[1][:, t - 2, :], picked[:, t, :], ALU.subtract)
+
+        za = [ps.tile([P, PACK, HALF], F32, name="za%d" % h) for h in range(2)]
+        for h in range(2):
+            cols = slice(h * HALF, (h + 1) * HALF)
+            for t in range(PACK):
+                nc.tensor.matmul_mx(
+                    out=za[h][:, t, :],
+                    lhsT=wa_dealt[:, t * P : (t + 1) * P].bitcast(E5M2),
+                    lhsT_scale=wa_scales_dealt[:, t * P : (t + 1) * P],
+                    rhs=xa_words[:, cols].bitcast(E4M3),
+                    rhs_scale=xa_scales[:, cols],
+                    start=True,
+                    stop=True,
+                )
+
+        hb = sb.tile([P, I * PACK], BF16, name="hb", align_bytes=64)
+        hb_scales = sb.tile([P, I], U8, name="hb_scales", align_bytes=64)
+        nc.scalar.activation(
+            hb[:].rearrange("p (c i t) -> p c t i", t=PACK, i=4),
+            diff[:].rearrange("p t (c i) -> p c t i", i=4),
+            ACT.Relu,
+        )
+
+        ha = [sb.tile([P, HALF * PACK], BF16, name="ha%d" % h, align_bytes=64) for h in range(2)]
+        ha_codes = [sb.tile([P, HALF], U32, name="ha_codes%d" % h, align_bytes=64) for h in range(2)]
+        ha_scales = [sb.tile([P, HALF], U8, name="ha_scales%d" % h, align_bytes=64) for h in range(2)]
+        for h in range(2):
+            nc.vector.tensor_tensor(
+                ha[h][:].rearrange("p (c i t) -> p c t i", t=PACK, i=4),
+                za[h][:].rearrange("p t (c i) -> p c t i", i=4),
+                oa_halves[h][:].rearrange("p t (c i) -> p c t i", i=4),
+                ALU.max,
+            )
+        nc.vector.quantize_mx(out=ha_codes[0][:].bitcast(E4M3), scales=ha_scales[0][:], in_=ha[0][:])
+        hb_codes = sb.tile([P, I], U32, name="hb_codes", tag="oa_half1", align_bytes=64)
+        nc.vector.quantize_mx(out=hb_codes[:].bitcast(E5M2), scales=hb_scales[:], in_=hb[:])
+        nc.vector.quantize_mx(out=ha_codes[1][:].bitcast(E4M3), scales=ha_scales[1][:], in_=ha[1][:])
+
+        met = [ps.tile([P, I], F32, name="met%d" % h) for h in range(2)]
+        for h in range(2):
+            nc.tensor.matmul_mx(
+                out=met[h][:],
+                lhsT=ha_codes[h][:].bitcast(E4M3),
+                lhsT_scale=ha_scales[h][:],
+                rhs=hb_codes[:].bitcast(E5M2),
+                rhs_scale=hb_scales[:],
+                start=True,
+                stop=True,
+            )
+
+        shares = sb.tile([P, I], F32, name="shares")
+        minus_mean = sb.tile([P, 1], F32, name="minus_mean")
+        kept0 = sb.tile([P, I], F32, name="kept0")
+        nc.scalar.activation(shares[:], met[0][:], ACT.Copy, scale=-KEEP / I, accum_out=minus_mean[:])
+        nc.scalar.activation(kept0[:], met[0][:], ACT.Relu, scale=KEEP, bias=minus_mean[:])
+        nc.sync.dma_start(out[0:HALF, :], kept0[:])
+
+        shares1 = sb.tile([P, I], F32, name="shares1")
+        minus_mean1 = sb.tile([P, 1], F32, name="minus_mean1")
+        kept1 = sb.tile([P, I], F32, name="kept1")
+        nc.vector.tensor_scalar(shares1[:], met[1][:], -KEEP / I, None, ALU.mult, ALU.add, accum_out=minus_mean1[:])
+        nc.scalar.activation(kept1[:], met[1][:], ACT.Relu, scale=KEEP, bias=minus_mean1[:])
+        nc.scalar.dma_start(out[HALF : 2 * HALF, :], kept1[:])

@@ -35,10 +35,10 @@ def load_scale_rows(queue, plane, scales):
         queue.dma_start(plane[32 * q : 32 * q + 4, :].bitcast(I32), rows[4 * q : 4 * q + 4, :])
 
 
-def deal_columns(copy, dealt, given):
+def deal_columns(copy, dealt, given, run):
     copy(
-        dealt.rearrange("p (t c i) -> p c t i", t=PACK, i=4),
-        given.rearrange("p (c i t) -> p c t i", t=PACK, i=4),
+        dealt.rearrange("p (t c i) -> p c t i", t=PACK, i=run),
+        given.rearrange("p (c i t) -> p c t i", t=PACK, i=run),
     )
 
 
@@ -79,8 +79,8 @@ def tile_list_meet_added_overtable_abovemean_kernel(
         nc.sync.dma_start(list_a[:], offs)
         load_scale_rows_filling(nc.sync, x_scales, xt_scales)
         nc.sync.dma_start(tb_pairs[0][:], tb_rows[:, 0 : 2 * V])
-        nc.sync.dma_start(list_t[:], offs3)
         nc.sync.dma_start(wb_given[:], wb_words[0].bitcast(I32))
+        nc.sync.dma_start(list_t[:], offs3)
         load_scale_rows(nc.sync, wb_scales_given, wb_scales)
         nc.sync.dma_start(tb_pairs[1][:], tb_rows[:, 2 * V : 4 * V])
         nc.sync.dma_start(wa_given[:], wa_words[0].rearrange("p c r -> p (c r)").bitcast(I32))
@@ -102,7 +102,7 @@ def tile_list_meet_added_overtable_abovemean_kernel(
         nc.vector.tensor_copy(xa_scales[:], x_scales[:].indirect(list_a[:]))
         deal_bytes(nc, wb_scales_dealt[:], wb_scales_given[:])
         wb_dealt = sb.tile([P, R], U16, name="wb_dealt", align_bytes=64)
-        deal_columns(nc.scalar.copy, wb_dealt[:], wb_given[:].bitcast(U16))
+        deal_columns(nc.scalar.copy, wb_dealt[:], wb_given[:].bitcast(U16), 8)
         zb = [ps.tile([P, 2, I], F32, name="zb%d" % u) for u in range(2)]
         wb_bytes = wb_dealt[:].bitcast(U8)
         for t in range(PACK):
@@ -121,12 +121,13 @@ def tile_list_meet_added_overtable_abovemean_kernel(
         for t in range(PACK):
             window = tb_pairs[t // 2][:, (t % 2) * V : (t % 2 + 1) * V]
             nc.scalar.activation(picked[:, t, :], window.indirect(list_t[:]), ACT.Copy)
-        deal_columns(nc.vector.tensor_copy, wa_dealt[:].bitcast(I32), wa_given[:])
+        diff_low = sb.tile([P, 2, I], F32, name="diff_low", align_bytes=64)
+        nc.vector.tensor_tensor(diff_low[:], zb[0][:], picked[:, 0:2, :], ALU.subtract)
+        deal_columns(nc.vector.tensor_copy, wa_dealt[:].bitcast(I32), wa_given[:], 4)
         deal_bytes(nc, wa_scales_dealt[:], wa_scales_given[:])
-        diff = sb.tile([P, PACK, I], F32, name="diff", tag="wa_scales_then_diff", align_bytes=64)
-        nc.vector.tensor_tensor(diff[:, 0:2, :], zb[0][:], picked[:, 0:2, :], ALU.subtract)
+        diff_high = sb.tile([P, 2, I], F32, name="diff_high", tag="wa_scales_then_diff", align_bytes=64)
         for t in (2, 3):
-            nc.vector.tensor_tensor(diff[:, t, :], zb[1][:, t - 2, :], picked[:, t, :], ALU.subtract)
+            nc.vector.tensor_tensor(diff_high[:, t - 2, :], zb[1][:, t - 2, :], picked[:, t, :], ALU.subtract)
 
         za = [ps.tile([P, PACK, HALF], F32, name="za%d" % h) for h in range(2)]
         for h in range(2):
@@ -144,24 +145,22 @@ def tile_list_meet_added_overtable_abovemean_kernel(
 
         hb = sb.tile([P, I * PACK], BF16, name="hb", align_bytes=64)
         hb_scales = sb.tile([P, I], U8, name="hb_scales", align_bytes=64)
-        nc.scalar.activation(
-            hb[:].rearrange("p (c i t) -> p c t i", t=PACK, i=4),
-            diff[:].rearrange("p t (c i) -> p c t i", i=4),
-            ACT.Relu,
-        )
+        hb_slots = hb[:].rearrange("p (c i t) -> p c t i", t=PACK, i=2)
+        for u, diff in enumerate((diff_low, diff_high)):
+            nc.scalar.activation(hb_slots[:, :, 2 * u : 2 * u + 2, :], diff[:].rearrange("p t (c i) -> p c t i", i=2), ACT.Relu)
 
         ha = [sb.tile([P, HALF * PACK], BF16, name="ha%d" % h, align_bytes=64) for h in range(2)]
         ha_codes = [sb.tile([P, HALF], U32, name="ha_codes%d" % h, align_bytes=64) for h in range(2)]
         ha_scales = [sb.tile([P, HALF], U8, name="ha_scales%d" % h, align_bytes=64) for h in range(2)]
         for h in range(2):
             nc.vector.tensor_tensor(
-                ha[h][:].rearrange("p (c i t) -> p c t i", t=PACK, i=4),
-                za[h][:].rearrange("p t (c i) -> p c t i", i=4),
-                oa_halves[h][:].rearrange("p t (c i) -> p c t i", i=4),
+                ha[h][:].rearrange("p (c i t) -> p c t i", t=PACK, i=2),
+                za[h][:].rearrange("p t (c i) -> p c t i", i=2),
+                oa_halves[h][:].rearrange("p t (c i) -> p c t i", i=2),
                 ALU.max,
             )
         nc.vector.quantize_mx(out=ha_codes[0][:].bitcast(E4M3), scales=ha_scales[0][:], in_=ha[0][:])
-        hb_codes = sb.tile([P, I], U32, name="hb_codes", tag="oa_half1", align_bytes=64)
+        hb_codes = sb.tile([P, I], U32, name="hb_codes", tag="oa_half0", align_bytes=64)
         nc.vector.quantize_mx(out=hb_codes[:].bitcast(E5M2), scales=hb_scales[:], in_=hb[:])
         nc.vector.quantize_mx(out=ha_codes[1][:].bitcast(E4M3), scales=ha_scales[1][:], in_=ha[1][:])
 

@@ -66,7 +66,7 @@ def tile_list_meet_added_overtable_abovemean_kernel(
         wb_given = sb.tile([P, R // 2], I32, name="wb_given", tag="wb_then_picked", align_bytes=64)
         wa_scales_given = sb.tile([P, R], U8, name="wa_scales_given", tag="wa_scales_then_diff", align_bytes=64)
         wb_scales_given = sb.tile([P, R], U8, name="wb_scales_given", align_bytes=64)
-        tb_pairs = [sb.tile([P, 2 * V], F32, name="tb_pair%d" % u, align_bytes=64) for u in range(2)]
+        tb_pairs = [sb.tile([P, 2 * V], F32, name="tb_pair%d" % u, tag="tb_pair%d" % u, align_bytes=64) for u in range(2)]
         oa_halves = [sb.tile([P, PACK, HALF], F32, name="oa_half%d" % h, tag="oa_half%d" % h, align_bytes=64) for h in range(2)]
 
         tb_rows = tb.rearrange("(p t) v -> p (t v)", t=PACK)
@@ -74,16 +74,16 @@ def tile_list_meet_added_overtable_abovemean_kernel(
 
         nc.vector.memset(wb_scales_given[:].bitcast(I32), 0)
         nc.vector.memset(wa_scales_given[:].bitcast(I32), 0)
+        nc.gpsimd.dma_start(tb_pairs[0][:], tb_rows[:, 0 : 2 * V])
         nc.sync.dma_start(list_b[:], offs2)
         nc.sync.dma_start(x_words[:], xt_words[0].rearrange("p c r -> p (c r)").bitcast(I32))
         nc.sync.dma_start(list_a[:], offs)
         load_scale_rows_filling(nc.sync, x_scales, xt_scales)
-        nc.sync.dma_start(tb_pairs[0][:], tb_rows[:, 0 : 2 * V])
         nc.sync.dma_start(wb_given[:], wb_words[0].bitcast(I32))
         nc.sync.dma_start(list_t[:], offs3)
         load_scale_rows(nc.sync, wb_scales_given, wb_scales)
-        nc.sync.dma_start(tb_pairs[1][:], tb_rows[:, 2 * V : 4 * V])
         nc.sync.dma_start(wa_given[:], wa_words[0].rearrange("p c r -> p (c r)").bitcast(I32))
+        nc.sync.dma_start(tb_pairs[1][:], tb_rows[:, 2 * V : 4 * V])
         load_scale_rows(nc.sync, wa_scales_given, wa_scales)
         for h in range(2):
             nc.sync.dma_start(oa_halves[h][:], oa_rows[:, :, h * HALF : (h + 1) * HALF])
@@ -143,13 +143,14 @@ def tile_list_meet_added_overtable_abovemean_kernel(
                     stop=True,
                 )
 
-        hb = sb.tile([P, I * PACK], BF16, name="hb", align_bytes=64)
+        hb = sb.tile([P, I * PACK], BF16, name="hb", tag="tb_pair1", align_bytes=64)
         hb_scales = sb.tile([P, I], U8, name="hb_scales", align_bytes=64)
         hb_slots = hb[:].rearrange("p (c i t) -> p c t i", t=PACK, i=2)
         for u, diff in enumerate((diff_low, diff_high)):
             nc.scalar.activation(hb_slots[:, :, 2 * u : 2 * u + 2, :], diff[:].rearrange("p t (c i) -> p c t i", i=2), ACT.Relu)
 
-        ha = [sb.tile([P, HALF * PACK], BF16, name="ha%d" % h, align_bytes=64) for h in range(2)]
+        ha_both = sb.tile([P, J * PACK], BF16, name="ha_both", tag="wb_then_picked", align_bytes=64)
+        ha = [ha_both[:, h * HALF * PACK : (h + 1) * HALF * PACK] for h in range(2)]
         ha_codes = [sb.tile([P, HALF], U32, name="ha_codes%d" % h, align_bytes=64) for h in range(2)]
         ha_scales = [sb.tile([P, HALF], U8, name="ha_scales%d" % h, align_bytes=64) for h in range(2)]
         for h in range(2):

from contextlib import ExitStack

import concourse.mybir as mybir

K, T, J, I, R, V = 512, 512, 256, 256, 512, 512
FLOPS = 2 * K * R * (J + I) + 2 * R * J * I

F32 = mybir.dt.float32
BF16 = mybir.dt.bfloat16
I32 = mybir.dt.int32
U32 = mybir.dt.uint32
U16 = mybir.dt.uint16
U8 = mybir.dt.uint8
E4M3 = mybir.dt.float8_e4m3fn_x4
E5M2 = mybir.dt.float8_e5m2_x4
E2M1 = mybir.dt.float4_e2m1fn_x4
ALU = mybir.AluOpType
ACT = mybir.ActivationFunctionType

P = 128
PACK = 4
HALF = 128
KEEP = 0.04


def load_scale_rows_filling(queue, plane, scales):
    rows = scales[0].bitcast(I32).rearrange("(q o r) c -> q o r c", o=1, r=4)
    for q in range(4):
        queue.dma_start(plane[32 * q : 32 * (q + 1), :].bitcast(I32), rows[q].broadcast_to([8, 4, rows.shape[3]]))


def load_scale_rows(queue, plane, scales):
    rows = scales[0].bitcast(I32)
    for q in range(4):
        queue.dma_start(plane[32 * q : 32 * q + 4, :].bitcast(I32), rows[4 * q : 4 * q + 4, :])


def deal_columns(copy, dealt, given, run):
    copy(
        dealt.rearrange("p (t c i) -> p c t i", t=PACK, i=run),
        given.rearrange("p (c i t) -> p c t i", t=PACK, i=run),
    )


def deal_bytes(nc, dealt, given):
    nc.vector.tensor_copy(
        dealt.rearrange("p (t c i) -> p c t i", t=PACK, i=16),
        given.rearrange("p (c i t) -> p c t i", t=PACK, i=16),
    )


def tile_list_meet_added_overtable_abovemean_kernel(
    tc, xt_words, xt_scales, wa_words, wa_scales, oa, wb_words, wb_scales, tb, offs, offs2, offs3, out
):
    nc = tc.nc
    with ExitStack() as ctx:
        sb = ctx.enter_context(tc.tile_pool(name="sb", bufs=1))
        ps = ctx.enter_context(tc.psum_pool(name="ps", bufs=1))

        list_a = sb.tile([P, J // 16], U16, name="list_a")
        list_b = sb.tile([P, I // 16], U16, name="list_b")
        list_t = sb.tile([P, I // 16], U16, name="list_t")
        x_scales = sb.tile([P, T], U8, name="x_scales", align_bytes=64)
        x_words = sb.tile([P, T], I32, name="x_words", align_bytes=64)
        wa_given = sb.tile([P, R], I32, name="wa_given", align_bytes=64)
        wb_given = sb.tile([P, R // 2], I32, name="wb_given", tag="wb_then_picked", align_bytes=64)
        wa_scales_given = sb.tile([P, R], U8, name="wa_scales_given", tag="wa_scales_then_diff", align_bytes=64)
        wb_scales_given = sb.tile([P, R], U8, name="wb_scales_given", align_bytes=64)
        tb_pairs = [sb.tile([P, 2 * V], F32, name="tb_pair%d" % u, tag="tb_pair%d" % u, align_bytes=64) for u in range(2)]
        oa_halves = [sb.tile([P, PACK, HALF], F32, name="oa_half%d" % h, tag="oa_half%d" % h, align_bytes=64) for h in range(2)]

        tb_rows = tb.rearrange("(p t) v -> p (t v)", t=PACK)
        oa_rows = oa.rearrange("(p t) j -> p t j", t=PACK)

        nc.vector.memset(wb_scales_given[:].bitcast(I32), 0)
        nc.vector.memset(wa_scales_given[:].bitcast(I32), 0)
        nc.gpsimd.dma_start(tb_pairs[0][:], tb_rows[:, 0 : 2 * V])
        nc.sync.dma_start(list_b[:], offs2)
        nc.sync.dma_start(x_words[:], xt_words[0].rearrange("p c r -> p (c r)").bitcast(I32))
        nc.sync.dma_start(list_a[:], offs)
        load_scale_rows_filling(nc.sync, x_scales, xt_scales)
        nc.sync.dma_start(wb_given[:], wb_words[0].bitcast(I32))
        nc.sync.dma_start(list_t[:], offs3)
        load_scale_rows(nc.sync, wb_scales_given, wb_scales)
        nc.sync.dma_start(wa_given[:], wa_words[0].rearrange("p c r -> p (c r)").bitcast(I32))
        nc.sync.dma_start(tb_pairs[1][:], tb_rows[:, 2 * V : 4 * V])
        load_scale_rows(nc.sync, wa_scales_given, wa_scales)
        for h in range(2):
            nc.sync.dma_start(oa_halves[h][:], oa_rows[:, :, h * HALF : (h + 1) * HALF])

        xb_scales = sb.tile([P, I], U8, name="xb_scales", align_bytes=64)
        xb_words = sb.tile([P, I], U32, name="xb_words", align_bytes=64)
        xa_scales = sb.tile([P, J], U8, name="xa_scales", align_bytes=64)
        xa_words = sb.tile([P, J], U32, name="xa_words", align_bytes=64)
        wa_dealt = sb.tile([P, R], U32, name="wa_dealt", align_bytes=64)
        wa_scales_dealt = sb.tile([P, R], U8, name="wa_scales_dealt", align_bytes=64)
        wb_scales_dealt = sb.tile([P, R], U8, name="wb_scales_dealt", align_bytes=64)

        nc.vector.tensor_copy(xb_words[:], x_words[:].bitcast(U32).indirect(list_b[:]))
        nc.vector.tensor_copy(xa_words[:], x_words[:].bitcast(U32).indirect(list_a[:]))
        nc.vector.tensor_copy(xb_scales[:], x_scales[:].indirect(list_b[:]))
        nc.vector.tensor_copy(xa_scales[:], x_scales[:].indirect(list_a[:]))
        deal_bytes(nc, wb_scales_dealt[:], wb_scales_given[:])
        wb_dealt = sb.tile([P, R], U16, name="wb_dealt", align_bytes=64)
        deal_columns(nc.scalar.copy, wb_dealt[:], wb_given[:].bitcast(U16), 8)
        zb = [ps.tile([P, 2, I], F32, name="zb%d" % u) for u in range(2)]
        wb_bytes = wb_dealt[:].bitcast(U8)
        for t in range(PACK):
            nc.tensor.matmul_mx(
                out=zb[t // 2][:, t % 2, :],
                lhsT=wb_bytes[:, 2 * t * P : 2 * (t + 1) * P].bitcast(E2M1),
                lhsT_scale=wb_scales_dealt[:, t * P : (t + 1) * P],
                rhs=xb_words[:].bitcast(E4M3),
                rhs_scale=xb_scales[:],
                start=True,
                stop=True,
            )


        picked = sb.tile([P, PACK, I], F32, name="picked", tag="wb_then_picked", align_bytes=64)
        for t in range(PACK):
            window = tb_pairs[t // 2][:, (t % 2) * V : (t % 2 + 1) * V]
            nc.scalar.activation(picked[:, t, :], window.indirect(list_t[:]), ACT.Copy)
        diff_low = sb.tile([P, 2, I], F32, name="diff_low", align_bytes=64)
        nc.vector.tensor_tensor(diff_low[:], zb[0][:], picked[:, 0:2, :], ALU.subtract)
        deal_columns(nc.vector.tensor_copy, wa_dealt[:].bitcast(I32), wa_given[:], 4)
        deal_bytes(nc, wa_scales_dealt[:], wa_scales_given[:])
        diff_high = sb.tile([P, 2, I], F32, name="diff_high", tag="wa_scales_then_diff", align_bytes=64)
        for t in (2, 3):
            nc.vector.tensor_tensor(diff_high[:, t - 2, :], zb[1][:, t - 2, :], picked[:, t, :], ALU.subtract)

        za = [ps.tile([P, PACK, HALF], F32, name="za%d" % h) for h in range(2)]
        for h in range(2):
            cols = slice(h * HALF, (h + 1) * HALF)
            for t in range(PACK):
                nc.tensor.matmul_mx(
                    out=za[h][:, t, :],
                    lhsT=wa_dealt[:, t * P : (t + 1) * P].bitcast(E5M2),
                    lhsT_scale=wa_scales_dealt[:, t * P : (t + 1) * P],
                    rhs=xa_words[:, cols].bitcast(E4M3),
                    rhs_scale=xa_scales[:, cols],
                    start=True,
                    stop=True,
                )

        hb = sb.tile([P, I * PACK], BF16, name="hb", tag="tb_pair1", align_bytes=64)
        hb_scales = sb.tile([P, I], U8, name="hb_scales", align_bytes=64)
        hb_slots = hb[:].rearrange("p (c i t) -> p c t i", t=PACK, i=2)
        for u, diff in enumerate((diff_low, diff_high)):
            nc.scalar.activation(hb_slots[:, :, 2 * u : 2 * u + 2, :], diff[:].rearrange("p t (c i) -> p c t i", i=2), ACT.Relu)

        ha_both = sb.tile([P, J * PACK], BF16, name="ha_both", tag="wb_then_picked", align_bytes=64)
        ha = [ha_both[:, h * HALF * PACK : (h + 1) * HALF * PACK] for h in range(2)]
        ha_codes = [sb.tile([P, HALF], U32, name="ha_codes%d" % h, align_bytes=64) for h in range(2)]
        ha_scales = [sb.tile([P, HALF], U8, name="ha_scales%d" % h, align_bytes=64) for h in range(2)]
        for h in range(2):
            nc.vector.tensor_tensor(
                ha[h][:].rearrange("p (c i t) -> p c t i", t=PACK, i=2),
                za[h][:].rearrange("p t (c i) -> p c t i", i=2),
                oa_halves[h][:].rearrange("p t (c i) -> p c t i", i=2),
                ALU.max,
            )
        nc.vector.quantize_mx(out=ha_codes[0][:].bitcast(E4M3), scales=ha_scales[0][:], in_=ha[0][:])
        hb_codes = sb.tile([P, I], U32, name="hb_codes", tag="oa_half0", align_bytes=64)
        nc.vector.quantize_mx(out=hb_codes[:].bitcast(E5M2), scales=hb_scales[:], in_=hb[:])
        nc.vector.quantize_mx(out=ha_codes[1][:].bitcast(E4M3), scales=ha_scales[1][:], in_=ha[1][:])

        met = [ps.tile([P, I], F32, name="met%d" % h) for h in range(2)]
        for h in range(2):
            nc.tensor.matmul_mx(
                out=met[h][:],
                lhsT=ha_codes[h][:].bitcast(E4M3),
                lhsT_scale=ha_scales[h][:],
                rhs=hb_codes[:].bitcast(E5M2),
                rhs_scale=hb_scales[:],
                start=True,
                stop=True,
            )

        shares = sb.tile([P, I], F32, name="shares")
        minus_mean = sb.tile([P, 1], F32, name="minus_mean")
        kept0 = sb.tile([P, I], F32, name="kept0")
        nc.scalar.activation(shares[:], met[0][:], ACT.Copy, scale=-KEEP / I, accum_out=minus_mean[:])
        nc.scalar.activation(kept0[:], met[0][:], ACT.Relu, scale=KEEP, bias=minus_mean[:])
        nc.sync.dma_start(out[0:HALF, :], kept0[:])

        shares1 = sb.tile([P, I], F32, name="shares1")
        minus_mean1 = sb.tile([P, 1], F32, name="minus_mean1")
        kept1 = sb.tile([P, I], F32, name="kept1")
        nc.vector.tensor_scalar(shares1[:], met[1][:], -KEEP / I, None, ALU.mult, ALU.add, accum_out=minus_mean1[:])
        nc.scalar.activation(kept1[:], met[1][:], ACT.Relu, scale=KEEP, bias=minus_mean1[:])
        nc.scalar.dma_start(out[HALF : 2 * HALF, :], kept1[:])
